import numpy as np
import ml_dtypes


def mxq(x, axis, fmt="e4m3"):
    dtype, down = {"e4m3": (ml_dtypes.float8_e4m3fn, 7), "e5m2": (ml_dtypes.float8_e5m2, 14)}[fmt]
    v = np.moveaxis(np.asarray(x, np.float32).astype(ml_dtypes.bfloat16).astype(np.float64), axis, -1)
    blocks = v.reshape(v.shape[:-1] + (-1, 32))
    amax = np.abs(blocks).max(-1, keepdims=True)
    byte = np.maximum(np.where(amax > 0, np.frexp(amax)[1] - 1 + 127, 0) - down, 1)
    scale = np.exp2(byte - 127.0)
    codes = (blocks / scale).astype(np.float32).astype(dtype).astype(np.float64)
    return np.moveaxis((codes * scale).reshape(v.shape), -1, axis)


WIDE = False


def mx_kscale(k):
    if not WIDE:
        return np.ones(k)
    levels = np.array([30, -30])
    if k % 512:
        return np.exp2(np.random.permutation(np.resize(levels, k // 32))).repeat(32)
    a = np.empty((k // 512, 16))
    for p in range(k // 512):
        a[p, :8] = np.random.permutation(np.resize(levels, 8))
        for g in range(8):
            far = levels[np.abs(levels - a[p, g]) >= 10]
            a[p, g + 8] = far[np.random.randint(len(far))]
    return np.exp2(a.ravel()).repeat(32)


def f64(x):
    return np.asarray(x).astype(np.float64)


def striped(idx):
    return np.tile(np.asarray(idx).reshape(-1, 16).T, (8, 1)).astype(np.uint16)


def unstriped(offs):
    return offs[:16].T.reshape(-1).astype(np.int64)


E2M1 = np.array([0.0, 0.5, 1.0, 1.5, 2.0, 3.0, 4.0, 6.0, -0.0, -0.5, -1.0, -1.5, -2.0, -3.0, -4.0, -6.0])


def pack_weight(w, fmt):
    k, n = w.shape
    w = f64(np.asarray(w, np.float32).astype(ml_dtypes.bfloat16)).reshape(k // 32, 32, n)
    amax = np.abs(w).max(1)
    if fmt in ("e4m3", "e5m2"):
        byte = np.frexp(amax)[1] - 1 + 127 - (7 if fmt == "e4m3" else 14)
    else:
        mant, ex = np.frexp(amax / 6.0)
        byte = np.where(mant > 0.5, ex, ex - 1) + 127
    byte = np.clip(np.where(amax > 0, byte, 1), 1, 254)
    scaled = (w * np.exp2(127.0 - byte)[:, None, :]).reshape(k, n).astype(np.float32)
    by_word = np.ascontiguousarray(scaled.reshape(k // 512, 128, 4, n).transpose(0, 1, 3, 2))
    if fmt in ("e4m3", "e5m2"):
        words = by_word.astype(ml_dtypes.float8_e4m3fn if fmt == "e4m3" else ml_dtypes.float8_e5m2).view(np.uint8)
    else:
        c = by_word.astype(ml_dtypes.float4_e2m1fn).view(np.uint8) & 0xF
        words = (c[..., 0::2] | (c[..., 1::2] << 4)).reshape(k // 512, 128, 2 * n)
    return np.ascontiguousarray(words), np.ascontiguousarray(byte.astype(np.uint8).reshape(k // 512, 16, n))


def unpack_weight(words, scales, fmt):
    g, _, n = scales.shape
    words = np.ascontiguousarray(words).reshape(g, 128, n, -1)
    if fmt in ("e4m3", "e5m2"):
        vals = words.view(ml_dtypes.float8_e4m3fn if fmt == "e4m3" else ml_dtypes.float8_e5m2).astype(np.float64)
    else:
        nib = np.empty((g, 128, n, 4), np.uint8)
        nib[..., 0::2] = words & 0xF
        nib[..., 1::2] = words >> 4
        vals = E2M1[nib]
    vals = vals * np.repeat(np.exp2(scales.astype(np.float64) - 127.0), 8, axis=1)[..., None]
    return vals.transpose(0, 1, 3, 2).reshape(g * 512, n)


def sigmoid(v):
    return 1.0 / (1.0 + np.exp(-v))


def bf(x):
    return np.asarray(x, np.float32).astype(ml_dtypes.bfloat16)


def planes(Y):
    r, m = Y.shape
    b = f64(bf(Y)).reshape(r // 32, 32, m)
    amax = np.abs(b).max(1)
    byte = np.clip(np.where(amax > 0, np.frexp(amax)[1] - 1 + 127 - 7, 1), 1, 254)
    codes = (b * np.exp2(127.0 - byte)[:, None, :]).reshape(r, m).astype(np.float32).astype(ml_dtypes.float8_e4m3fn).view(np.uint8)
    words = codes.reshape(r // 512, 128, 4, m).transpose(0, 1, 3, 2)
    return np.ascontiguousarray(words), np.ascontiguousarray(byte.astype(np.uint8).reshape(r // 512, 16, m))


K, T, J, R, F, Z, N, M = 512, 512, 256, 512, 512, 1024, 512, 512


def setup_inputs():
    n = np.random.standard_normal
    idx = np.random.permutation(T)[:J]
    idx2 = np.random.permutation(Z)[:J]
    idx3 = np.random.permutation(M)[:J]
    fk = mx_kscale(K)
    fr = mx_kscale(R)
    ff = mx_kscale(F)
    xtp = pack_weight(n((K, T)) / fk[:, None], "e2m1")
    wp = pack_weight(n((K, R)) * 1 / np.sqrt(K) * fk[:, None] * fr, "e5m2")
    w2p = pack_weight(n((F, R)) * 1 / np.sqrt(F) * ff[:, None] * fr, "e5m2")
    wbp = pack_weight(n((R, N)) * 1 / np.sqrt(R) / fr[:, None], "e4m3")
    return {
        "xt_words": xtp[0],
        "xt_scales": xtp[1],
        "w_words": wp[0],
        "w_scales": wp[1],
        "xo": (n((F, Z))).astype(np.float32),
        "fl": (np.random.uniform(0.5, 2.0, (F, 1)) / ff[:, None]).astype(np.float32),
        "so": (n((F, J))).astype(np.float32),
        "w2_words": w2p[0],
        "w2_scales": w2p[1],
        "wb_words": wbp[0],
        "wb_scales": wbp[1],
        "tz": (n((N, M)) * 0.6).astype(np.float32),
        "rw": (np.random.uniform(0.5, 2.0, (1, J))).astype(np.float32),
        "offs": striped(idx),
        "offs2": striped(idx2),
        "offs3": striped(idx3),
    }


def reference(xt_words, xt_scales, w_words, w_scales, xo, fl, so, w2_words, w2_scales, wb_words, wb_scales, tz, rw, offs, offs2, offs3):
    idx = unstriped(offs)
    idx2 = unstriped(offs2)
    idx3 = unstriped(offs3)
    xtu = unpack_weight(xt_words, xt_scales, "e2m1")
    wu = unpack_weight(w_words, w_scales, "e5m2")
    w2u = unpack_weight(w2_words, w2_scales, "e5m2")
    wbu = unpack_weight(wb_words, wb_scales, "e4m3")
    u2 = f64(xo)[:, idx2] * sigmoid(f64(so)) * f64(fl)
    xtidxg = xtu[:, idx]
    a = wu.T @ xtidxg
    u2q = mxq(u2, 0, "e4m3")
    q = w2u.T @ u2q
    y1 = np.pad(q, ((0, 0), (1, 0)))[:, :J]
    hid = np.maximum(a, q - 0.6 * y1)
    hidq = mxq(hid, 0, "e5m2")
    p = wbu.T @ hidq
    y = np.maximum(p, f64(tz)[:, idx3]) * f64(rw)
    words, scales = planes(y)
    return y, words, scales

@@ -1,0 +1,213 @@
+from contextlib import ExitStack
+
+import concourse.mybir as mybir
+from concourse.masks import make_identity
+
+K, T, J, R, F, Z, N, M = 512, 512, 256, 512, 512, 1024, 512, 512
+FLOPS = 2 * J * (K * R + F * R + R * N)
+
+F32 = mybir.dt.float32
+BF16 = mybir.dt.bfloat16
+I32 = mybir.dt.int32
+U16 = mybir.dt.uint16
+U8 = mybir.dt.uint8
+E4M3 = mybir.dt.float8_e4m3fn_x4
+E5M2 = mybir.dt.float8_e5m2_x4
+E2M1 = mybir.dt.float4_e2m1fn_x4
+ALU = mybir.AluOpType
+ACT = mybir.ActivationFunctionType
+
+P = 128
+PACK = 4
+HALF = J // 2
+LIST_COLS = J // 16
+STEP = 0.6
+
+
+def tile_list_two_picked_gated_stepgap_floored_pl_kernel(
+    tc, xt_words, xt_scales, w_words, w_scales, xo, fl, so, w2_words, w2_scales,
+    wb_words, wb_scales, tz, rw, offs, offs2, offs3, out_0, out_1, out_2,
+):
+    nc = tc.nc
+    halves = [slice(h * HALF, (h + 1) * HALF) for h in range(2)]
+
+    with ExitStack() as ctx:
+        sb = ctx.enter_context(tc.tile_pool(name="sb", bufs=1))
+        ps = ctx.enter_context(tc.psum_pool(name="ps", bufs=1))
+
+        def sbuf(name, shape, dtype, tag=None):
+            return sb.tile(shape, dtype, name=name, tag=tag or name, align_bytes=64)
+
+        def word_rows(words):
+            return words[0].rearrange("p c r -> p (c r)").bitcast(I32)
+
+        list_xt = sbuf("list_xt", [P, LIST_COLS], U16)
+        list_xo = sbuf("list_xo", [P, LIST_COLS], U16)
+        list_tz = sbuf("list_tz", [P, LIST_COLS], U16)
+
+        raw_scales = sbuf("raw_scales", [P, 3 * R], U8, tag="raw")
+        xt_scale_rows = sbuf("xt_scale_rows", [P, T], U8)
+        nc.vector.memset(xt_scale_rows[:].bitcast(I32), 0)
+        nc.vector.memset(raw_scales[:].bitcast(I32), 0)
+
+        nc.sync.dma_start(list_xt[:], offs)
+        nc.sync.dma_start(list_xo[:], offs2)
+        nc.sync.dma_start(list_tz[:], offs3)
+        so_sb = sbuf("so_sb", [P, PACK * J], F32)
+        nc.sync.dma_start(so_sb[:], so.rearrange("(p t) j -> p (t j)", t=PACK))
+        xo_rows = xo.rearrange("(p t) z -> p t z", t=PACK)
+        xo_sb = [sbuf(f"xo_sb{t}", [P, Z], F32) for t in range(PACK)]
+        nc.sync.dma_start(xo_sb[0][:], xo_rows[:, 0, :])
+        nc.scalar.dma_start(xt_scale_rows[0:16, :].bitcast(I32), xt_scales[0].bitcast(I32))
+        for i, src in enumerate((w2_scales, w_scales, wb_scales)):
+            nc.scalar.dma_start(raw_scales[0:16, i * R : (i + 1) * R].bitcast(I32), src[0].bitcast(I32))
+        xt_sb = sbuf("xt_sb", [P, T], U16)
+        nc.sync.dma_start(xt_sb[:].bitcast(I32), xt_words[0].bitcast(I32))
+        nc.sync.dma_start(xo_sb[1][:], xo_rows[:, 1, :])
+        nc.sync.dma_start(xo_sb[2][:], xo_rows[:, 2, :])
+        nc.sync.dma_start(xo_sb[3][:], xo_rows[:, 3, :])
+        fl_sb = sbuf("fl_sb", [P, PACK], F32)
+        nc.gpsimd.dma_start(fl_sb[:], fl.rearrange("(p t) o -> p (t o)", t=PACK))
+        rw_cols = sbuf("rw_cols", [P, 2], F32)
+        with nc.allow_non_contiguous_dma(reason="one slot weight to a partition"):
+            nc.gpsimd.dma_start(rw_cols[:], rw.rearrange("o (h p) -> p (o h)", h=2))
+
+        planes = sbuf("planes", [P, 3 * R + J], U8)
+        xt_scale_picked = sbuf("xt_scale_picked", [P, J], U8)
+        nc.vector.tensor_copy(xt_scale_picked[:], xt_scale_rows[:].indirect(list_xt[:]))
+        nc.vector.tensor_copy(planes[:, 3 * R :].bitcast(I32), xt_scale_picked[:].bitcast(I32))
+        nc.vector.tensor_copy(
+            planes[:, 0 : 3 * R].rearrange("p (w t m) -> p w t m", w=3, t=PACK),
+            raw_scales[:].rearrange("p (w m t) -> p w t m", w=3, t=PACK),
+        )
+        for q in range(1, 4):
+            nc.scalar.dma_start(planes[32 * q : 32 * q + 4, :].bitcast(I32), planes[4 * q : 4 * q + 4, :].bitcast(I32))
+        w2_plane, w_plane, wb_plane = [planes[:, i * R : (i + 1) * R] for i in range(3)]
+        xt_plane = planes[:, 3 * R :]
+
+        xt_picked = sbuf("xt_picked", [P, J], U16)
+        nc.vector.tensor_copy(xt_picked[:], xt_sb[:].indirect(list_xt[:]))
+
+        ident = sbuf("ident", [P, P], F32)
+        make_identity(nc, ident[:])
+        rw_ps = ps.tile([P, J], F32, name="rw_ps")
+        for h in range(2):
+            nc.tensor.transpose(rw_ps[:, halves[h]], rw_cols[:, h : h + 1].to_broadcast([P, P]), ident[:])
+
+        gate = sbuf("gate", [P, PACK * J], F32)
+        nc.scalar.activation(gate[:], so_sb[:], ACT.Sigmoid)
+        last = PACK - 1
+        gate_last = sbuf("gate_last", [P, J], F32)
+        nc.scalar.activation(gate_last[:], gate[:, last * J :], ACT.Copy, scale=fl_sb[:, last : last + 1])
+        u2 = sbuf("u2", [P, PACK, J], F32)
+        for t in range(last):
+            xo_picked = sbuf(f"xo_picked{t}", [P, J], F32)
+            nc.scalar.activation(xo_picked[:], xo_sb[t][:].indirect(list_xo[:]), ACT.Copy)
+            nc.vector.scalar_tensor_tensor(
+                u2[:, t, :], xo_picked[:], fl_sb[:, t : t + 1], gate[:, t * J : (t + 1) * J], ALU.mult, ALU.mult
+            )
+        for h in range(2):
+            cols = slice(h * LIST_COLS // 2, (h + 1) * LIST_COLS // 2)
+            nc.vector.tensor_tensor(
+                u2[:, last, halves[h]], xo_sb[last][:].indirect(list_xo[:, cols]), gate_last[:, halves[h]], ALU.mult
+            )
+
+        w2_raw = sbuf("w2_raw", [P, R], I32, tag="raw")
+        w_raw = sbuf("w_raw", [P, R], I32, tag="xt_sb")
+        wb_raw = sbuf("wb_raw", [P, N], I32, tag="so_sb")
+        tz_rows = tz.rearrange("(p u t) m -> p u (t m)", u=2, t=2)
+        tz_sb = [sbuf(f"tz_sb{u}", [P, 2 * M], F32, tag=f"xo_sb{u}") for u in range(2)]
+        nc.sync.dma_start(w2_raw[:], word_rows(w2_words))
+        nc.sync.dma_start(w_raw[:], word_rows(w_words))
+        nc.sync.dma_start(wb_raw[:], word_rows(wb_words))
+        for u in range(2):
+            nc.sync.dma_start(tz_sb[u][:], tz_rows[:, u, :])
+
+        def deal_columns(name, raw):
+            dealt = sbuf(name, [P, R], I32)
+            nc.vector.tensor_copy(
+                dealt[:].rearrange("p (t m) -> p t m", t=PACK), raw[:].rearrange("p (m t) -> p t m", t=PACK)
+            )
+            return dealt
+
+        def round_and_weave(name, src):
+            woven = sbuf(name, [P, HALF * PACK], BF16)
+            nc.scalar.copy(
+                woven[:].rearrange("p (c i t) -> p c t i", i=4, t=PACK), src.rearrange("p t (c i) -> p c t i", i=4)
+            )
+            return woven
+
+        def product(name, w_dealt, w_pl, w_fmt, codes, code_scales):
+            bank = ps.tile([P, PACK, HALF], F32, name=name)
+            for t in range(PACK):
+                cols = slice(t * P, (t + 1) * P)
+                nc.tensor.matmul_mx(
+                    out=bank[:, t, :], lhsT=w_dealt[:, cols].bitcast(w_fmt), lhsT_scale=w_pl[:, cols],
+                    rhs=codes, rhs_scale=code_scales, start=True, stop=True,
+                )
+            return bank
+
+        def woven_view(bank):
+            return bank[:].rearrange("p t j -> p j t")
+
+        u2_woven = [round_and_weave(f"u2_woven{h}", u2[:, :, halves[h]]) for h in range(2)]
+        w2_dealt = deal_columns("w2_dealt", w2_raw)
+        q_ps = []
+        for h in range(2):
+            codes = sbuf(f"u2_codes{h}", [P, HALF], I32)
+            scales = sbuf(f"u2_scales{h}", [P, HALF], U8)
+            nc.vector.quantize_mx(out=codes[:].bitcast(E4M3), scales=scales[:], in_=u2_woven[h][:])
+            q_ps.append(product(f"q_ps{h}", w2_dealt, w2_plane, E5M2, codes[:].bitcast(E4M3), scales[:]))
+
+        w_dealt = deal_columns("w_dealt", w_raw)
+        a_ps = [
+            product(f"a_ps{h}", w_dealt, w_plane, E5M2, xt_picked[:, halves[h]].bitcast(E2M1), xt_plane[:, halves[h]])
+            for h in range(2)
+        ]
+        wb_dealt = deal_columns("wb_dealt", wb_raw)
+
+        before = sbuf("before", [P, J, PACK], F32)
+        nc.vector.memset(before[:, 0, :], 0.0)
+        nc.scalar.activation(before[:, 1 : HALF + 1, :], woven_view(q_ps[0]), ACT.Copy, scale=-STEP)
+        nc.scalar.activation(before[:, HALF + 1 :, :], woven_view(q_ps[1])[:, 0 : HALF - 1, :], ACT.Copy, scale=-STEP)
+
+        tz_picked = sbuf("tz_picked", [P, PACK, J], F32)
+        for t in range(PACK):
+            window = tz_sb[t // 2][:, (t % 2) * M : (t % 2 + 1) * M]
+            nc.scalar.activation(tz_picked[:, t, :], window.indirect(list_tz[:]), ACT.Copy)
+
+        stepped = [sbuf(f"stepped{h}", [P, HALF, PACK], F32) for h in range(2)]
+        hid = [sbuf(f"hid{h}", [P, HALF, PACK], BF16) for h in range(2)]
+        for h in range(2):
+            nc.vector.tensor_tensor(stepped[h][:], woven_view(q_ps[h]), before[:, halves[h], :], ALU.add)
+        for h in range(2):
+            nc.vector.tensor_tensor(hid[h][:], woven_view(a_ps[h]), stepped[h][:], ALU.max)
+        p_ps = []
+        for h in range(2):
+            codes = sbuf(f"hid_codes{h}", [P, HALF], I32)
+            scales = sbuf(f"hid_scales{h}", [P, HALF], U8)
+            nc.vector.quantize_mx(
+                out=codes[:].bitcast(E5M2), scales=scales[:], in_=hid[h][:].rearrange("p j t -> p (j t)")
+            )
+            p_ps.append(product(f"p_ps{h}", wb_dealt, wb_plane, E4M3, codes[:].bitcast(E5M2), scales[:]))
+
+        floored = [sbuf(f"floored{h}", [P, PACK, HALF], F32) for h in range(2)]
+        y = [sbuf(f"y{h}", [P, PACK, HALF], F32) for h in range(2)]
+        out_rows = out_0.rearrange("(p t) j -> p t j", t=PACK)
+        y_codes = sbuf("y_codes", [P, J], I32)
+        y_scales = sbuf("y_scales", [P, J], U8)
+        for h in range(2):
+            nc.vector.tensor_tensor(floored[h][:], p_ps[h][:], tz_picked[:, :, halves[h]], ALU.max)
+        for h in range(2):
+            rw_all = rw_ps[:, halves[h]].unsqueeze(1).to_broadcast([P, PACK, HALF])
+            nc.vector.tensor_tensor(y[h][:], floored[h][:], rw_all, ALU.mult)
+            nc.sync.dma_start(out_rows[:, :, halves[h]], y[h][:])
+        for h in range(2):
+            y_woven = round_and_weave(f"y_woven{h}", y[h][:])
+            nc.vector.quantize_mx(
+                out=y_codes[:, halves[h]].bitcast(E4M3), scales=y_scales[:, halves[h]], in_=y_woven[:]
+            )
+        nc.sync.dma_start(word_rows(out_1), y_codes[:])
+        for q in range(4):
+            queue = nc.scalar if q % 2 == 0 else nc.sync
+            queue.dma_start(out_2[0, 4 * q : 4 * q + 4, :].bitcast(I32), y_scales[32 * q : 32 * q + 4, :].bitcast(I32))

@@ -22,6 +22,7 @@ PACK = 4
 HALF = J // 2
 LIST_COLS = J // 16
 STEP = 0.6
+SPLIT = 48
 
 
 def tile_list_two_picked_gated_stepgap_floored_pl_kernel(
@@ -47,27 +48,32 @@ def tile_list_two_picked_gated_stepgap_floored_pl_kernel(
 
         raw_scales = sbuf("raw_scales", [P, 3 * R], U8, tag="raw")
         xt_scale_rows = sbuf("xt_scale_rows", [P, T], U8)
-        nc.vector.memset(xt_scale_rows[:].bitcast(I32), 0)
-        nc.vector.memset(raw_scales[:].bitcast(I32), 0)
+        nc.gpsimd.memset(xt_scale_rows[:].bitcast(I32), 0)
+        nc.gpsimd.memset(raw_scales[:].bitcast(I32), 0)
 
-        nc.sync.dma_start(list_xt[:], offs)
-        nc.sync.dma_start(list_xo[:], offs2)
-        nc.sync.dma_start(list_tz[:], offs3)
         so_sb = sbuf("so_sb", [P, PACK * J], F32)
-        nc.sync.dma_start(so_sb[:], so.rearrange("(p t) j -> p (t j)", t=PACK))
         xo_rows = xo.rearrange("(p t) z -> p t z", t=PACK)
-        xo_sb = [sbuf(f"xo_sb{t}", [P, Z], F32) for t in range(PACK)]
-        nc.sync.dma_start(xo_sb[0][:], xo_rows[:, 0, :])
-        nc.scalar.dma_start(xt_scale_rows[0:16, :].bitcast(I32), xt_scales[0].bitcast(I32))
-        for i, src in enumerate((w2_scales, w_scales, wb_scales)):
-            nc.scalar.dma_start(raw_scales[0:16, i * R : (i + 1) * R].bitcast(I32), src[0].bitcast(I32))
+        xo_first = sbuf("xo_first", [P, 2 * Z], F32)
+        xo_third = sbuf("xo_third", [P, Z], F32)
+        xo_last = sbuf("xo_last", [P, Z], F32)
+        xo_planes = [xo_first[:, 0:Z], xo_first[:, Z:], xo_third[:], xo_last[:]]
         xt_sb = sbuf("xt_sb", [P, T], U16)
-        nc.sync.dma_start(xt_sb[:].bitcast(I32), xt_words[0].bitcast(I32))
-        nc.sync.dma_start(xo_sb[1][:], xo_rows[:, 1, :])
-        nc.sync.dma_start(xo_sb[2][:], xo_rows[:, 2, :])
-        nc.sync.dma_start(xo_sb[3][:], xo_rows[:, 3, :])
+        w2_raw = sbuf("w2_raw", [P, R], I32)
+        nc.sync.dma_start(so_sb[:], so.rearrange("(p t) j -> p (t j)", t=PACK))
+        nc.sync.dma_start(list_xt[:], offs)
+        nc.scalar.dma_start(xt_scale_rows[0:16, :].bitcast(I32), xt_scales[0].bitcast(I32))
+        for i, (src, queue) in enumerate(((w2_scales, nc.scalar), (w_scales, nc.scalar), (wb_scales, nc.sync))):
+            queue.dma_start(raw_scales[0:16, i * R : (i + 1) * R].bitcast(I32), src[0].bitcast(I32))
+        nc.sync.dma_start(xo_first[:], xo_rows[:, 0:2, :].rearrange("p t z -> p (t z)"))
+        nc.sync.dma_start(list_xo[:], offs2)
         fl_sb = sbuf("fl_sb", [P, PACK], F32)
-        nc.gpsimd.dma_start(fl_sb[:], fl.rearrange("(p t) o -> p (t o)", t=PACK))
+        nc.sync.dma_start(fl_sb[:], fl.rearrange("(p t) o -> p (t o)", t=PACK))
+        nc.sync.dma_start(xt_sb[:].bitcast(I32), xt_words[0].bitcast(I32))
+        nc.sync.dma_start(xo_third[:], xo_rows[:, 2, :])
+        nc.sync.dma_start(xo_last[:], xo_rows[:, 3, :])
+        nc.sync.dma_start(w2_raw[:], word_rows(w2_words))
+        nc.sync.dma_start(list_tz[:], offs3)
+
         rw_cols = sbuf("rw_cols", [P, 2], F32)
         with nc.allow_non_contiguous_dma(reason="one slot weight to a partition"):
             nc.gpsimd.dma_start(rw_cols[:], rw.rearrange("o (h p) -> p (o h)", h=2))
@@ -77,11 +83,11 @@ def tile_list_two_picked_gated_stepgap_floored_pl_kernel(
         nc.vector.tensor_copy(xt_scale_picked[:], xt_scale_rows[:].indirect(list_xt[:]))
         nc.vector.tensor_copy(planes[:, 3 * R :].bitcast(I32), xt_scale_picked[:].bitcast(I32))
         nc.vector.tensor_copy(
-            planes[:, 0 : 3 * R].rearrange("p (w t m) -> p w t m", w=3, t=PACK),
-            raw_scales[:].rearrange("p (w m t) -> p w t m", w=3, t=PACK),
+            planes[:, 0 : 3 * R].rearrange("p (w t m) -> p t w m", w=3, t=PACK),
+            raw_scales[:].rearrange("p (w m t) -> p t w m", w=3, t=PACK),
         )
         for q in range(1, 4):
-            nc.scalar.dma_start(planes[32 * q : 32 * q + 4, :].bitcast(I32), planes[4 * q : 4 * q + 4, :].bitcast(I32))
+            nc.sync.dma_start(planes[32 * q : 32 * q + 4, :].bitcast(I32), planes[4 * q : 4 * q + 4, :].bitcast(I32))
         w2_plane, w_plane, wb_plane = [planes[:, i * R : (i + 1) * R] for i in range(3)]
         xt_plane = planes[:, 3 * R :]
 
@@ -98,44 +104,43 @@ def tile_list_two_picked_gated_stepgap_floored_pl_kernel(
         nc.scalar.activation(gate[:], so_sb[:], ACT.Sigmoid)
         last = PACK - 1
         gate_last = sbuf("gate_last", [P, J], F32)
-        nc.scalar.activation(gate_last[:], gate[:, last * J :], ACT.Copy, scale=fl_sb[:, last : last + 1])
-        u2 = sbuf("u2", [P, PACK, J], F32)
+        nc.vector.tensor_scalar(gate_last[:], gate[:, last * J :], fl_sb[:, last : last + 1], None, ALU.mult)
+        u2 = sbuf("u2", [P, 2, PACK, HALF], F32)
         for t in range(last):
             xo_picked = sbuf(f"xo_picked{t}", [P, J], F32)
-            nc.scalar.activation(xo_picked[:], xo_sb[t][:].indirect(list_xo[:]), ACT.Copy)
+            nc.scalar.activation(xo_picked[:], xo_planes[t].indirect(list_xo[:]), ACT.Copy)
             nc.vector.scalar_tensor_tensor(
-                u2[:, t, :], xo_picked[:], fl_sb[:, t : t + 1], gate[:, t * J : (t + 1) * J], ALU.mult, ALU.mult
+                u2[:, :, t, :],
+                xo_picked[:].rearrange("p (h j) -> p h j", h=2),
+                fl_sb[:, t : t + 1],
+                gate[:, t * J : (t + 1) * J].rearrange("p (h j) -> p h j", h=2),
+                ALU.mult,
+                ALU.mult,
             )
         for h in range(2):
             cols = slice(h * LIST_COLS // 2, (h + 1) * LIST_COLS // 2)
             nc.vector.tensor_tensor(
-                u2[:, last, halves[h]], xo_sb[last][:].indirect(list_xo[:, cols]), gate_last[:, halves[h]], ALU.mult
+                u2[:, h, last, :], xo_planes[last].indirect(list_xo[:, cols]), gate_last[:, halves[h]], ALU.mult
             )
 
-        w2_raw = sbuf("w2_raw", [P, R], I32, tag="raw")
-        w_raw = sbuf("w_raw", [P, R], I32, tag="xt_sb")
-        wb_raw = sbuf("wb_raw", [P, N], I32, tag="so_sb")
+        late_raw = sbuf("late_raw", [P, R + N], I32, tag="raw")
+        w_raw, wb_raw = late_raw[:, 0:R], late_raw[:, R:]
         tz_rows = tz.rearrange("(p u t) m -> p u (t m)", u=2, t=2)
-        tz_sb = [sbuf(f"tz_sb{u}", [P, 2 * M], F32, tag=f"xo_sb{u}") for u in range(2)]
-        nc.sync.dma_start(w2_raw[:], word_rows(w2_words))
-        nc.sync.dma_start(w_raw[:], word_rows(w_words))
-        nc.sync.dma_start(wb_raw[:], word_rows(wb_words))
+        tz_sb = [sbuf(f"tz_sb{u}", [P, 2 * M], F32, tag=tag) for u, tag in enumerate(("xo_first", "xo_third"))]
+        nc.sync.dma_start(w_raw, word_rows(w_words))
+        nc.sync.dma_start(wb_raw, word_rows(wb_words))
         for u in range(2):
             nc.sync.dma_start(tz_sb[u][:], tz_rows[:, u, :])
 
-        def deal_columns(name, raw):
-            dealt = sbuf(name, [P, R], I32)
+        def deal_columns(name, raw, tag=None):
+            dealt = sbuf(name, [P, R], I32, tag=tag)
             nc.vector.tensor_copy(
-                dealt[:].rearrange("p (t m) -> p t m", t=PACK), raw[:].rearrange("p (m t) -> p t m", t=PACK)
+                dealt[:].rearrange("p (t m) -> p t m", t=PACK), raw.rearrange("p (m t) -> p t m", t=PACK)
             )
             return dealt
 
-        def round_and_weave(name, src):
-            woven = sbuf(name, [P, HALF * PACK], BF16)
-            nc.scalar.copy(
-                woven[:].rearrange("p (c i t) -> p c t i", i=4, t=PACK), src.rearrange("p t (c i) -> p c t i", i=4)
-            )
-            return woven
+        def round_and_weave(copy, woven, src):
+            copy(woven.rearrange("p (c i t) -> p c t i", i=4, t=PACK), src.rearrange("p t (c i) -> p c t i", i=4))
 
         def product(name, w_dealt, w_pl, w_fmt, codes, code_scales):
             bank = ps.tile([P, PACK, HALF], F32, name=name)
@@ -150,8 +155,10 @@ def tile_list_two_picked_gated_stepgap_floored_pl_kernel(
         def woven_view(bank):
             return bank[:].rearrange("p t j -> p j t")
 
-        u2_woven = [round_and_weave(f"u2_woven{h}", u2[:, :, halves[h]]) for h in range(2)]
-        w2_dealt = deal_columns("w2_dealt", w2_raw)
+        u2_woven = [sbuf(f"u2_woven{h}", [P, HALF * PACK], BF16) for h in range(2)]
+        for h in range(2):
+            round_and_weave(nc.scalar.copy, u2_woven[h][:], u2[:, h, :, :])
+        w2_dealt = deal_columns("w2_dealt", w2_raw[:])
         q_ps = []
         for h in range(2):
             codes = sbuf(f"u2_codes{h}", [P, HALF], I32)
@@ -159,7 +166,7 @@ def tile_list_two_picked_gated_stepgap_floored_pl_kernel(
             nc.vector.quantize_mx(out=codes[:].bitcast(E4M3), scales=scales[:], in_=u2_woven[h][:])
             q_ps.append(product(f"q_ps{h}", w2_dealt, w2_plane, E5M2, codes[:].bitcast(E4M3), scales[:]))
 
-        w_dealt = deal_columns("w_dealt", w_raw)
+        w_dealt = deal_columns("w_dealt", w_raw, tag="u2_woven1")
         a_ps = [
             product(f"a_ps{h}", w_dealt, w_plane, E5M2, xt_picked[:, halves[h]].bitcast(E2M1), xt_plane[:, halves[h]])
             for h in range(2)
@@ -202,10 +209,13 @@ def tile_list_two_picked_gated_stepgap_floored_pl_kernel(
             rw_all = rw_ps[:, halves[h]].unsqueeze(1).to_broadcast([P, PACK, HALF])
             nc.vector.tensor_tensor(y[h][:], floored[h][:], rw_all, ALU.mult)
             nc.sync.dma_start(out_rows[:, :, halves[h]], y[h][:])
+        y_woven = [sbuf(f"y_woven{h}", [P, HALF * PACK], BF16) for h in range(2)]
+        round_and_weave(nc.scalar.copy, y_woven[0][:], y[0][:])
+        round_and_weave(nc.scalar.copy, y_woven[1][:, 0 : SPLIT * PACK], y[1][:, :, 0:SPLIT])
+        round_and_weave(nc.vector.tensor_copy, y_woven[1][:, SPLIT * PACK :], y[1][:, :, SPLIT:])
         for h in range(2):
-            y_woven = round_and_weave(f"y_woven{h}", y[h][:])
             nc.vector.quantize_mx(
-                out=y_codes[:, halves[h]].bitcast(E4M3), scales=y_scales[:, halves[h]], in_=y_woven[:]
+                out=y_codes[:, halves[h]].bitcast(E4M3), scales=y_scales[:, halves[h]], in_=y_woven[h][:]
             )
         nc.sync.dma_start(word_rows(out_1), y_codes[:])
         for q in range(4):

@@ -23,6 +23,7 @@ HALF = J // 2
 LIST_COLS = J // 16
 STEP = 0.6
 SPLIT = 48
+LEAD = 4
 
 
 def tile_list_two_picked_gated_stepgap_floored_pl_kernel(
@@ -135,7 +136,8 @@ def tile_list_two_picked_gated_stepgap_floored_pl_kernel(
         def deal_columns(name, raw, tag=None):
             dealt = sbuf(name, [P, R], I32, tag=tag)
             nc.vector.tensor_copy(
-                dealt[:].rearrange("p (t m) -> p t m", t=PACK), raw.rearrange("p (m t) -> p t m", t=PACK)
+                dealt[:].rearrange("p (t c i) -> p c t i", t=PACK, i=4),
+                raw.rearrange("p (c i t) -> p c t i", t=PACK, i=4),
             )
             return dealt
 
@@ -151,9 +153,6 @@ def tile_list_two_picked_gated_stepgap_floored_pl_kernel(
                     rhs=codes, rhs_scale=code_scales, start=True, stop=True,
                 )
             return bank
-
-        def woven_view(bank):
-            return bank[:].rearrange("p t j -> p j t")
 
         u2_woven = [sbuf(f"u2_woven{h}", [P, HALF * PACK], BF16) for h in range(2)]
         for h in range(2):
@@ -173,29 +172,33 @@ def tile_list_two_picked_gated_stepgap_floored_pl_kernel(
         ]
         wb_dealt = deal_columns("wb_dealt", wb_raw)
 
-        before = sbuf("before", [P, J, PACK], F32)
-        nc.vector.memset(before[:, 0, :], 0.0)
-        nc.scalar.activation(before[:, 1 : HALF + 1, :], woven_view(q_ps[0]), ACT.Copy, scale=-STEP)
-        nc.scalar.activation(before[:, HALF + 1 :, :], woven_view(q_ps[1])[:, 0 : HALF - 1, :], ACT.Copy, scale=-STEP)
+        before = sbuf("before", [P, PACK, LEAD + J], F32)
+        nc.vector.memset(before[:, :, LEAD - 1 : LEAD], 0.0)
+        nc.scalar.activation(before[:, :, LEAD : LEAD + HALF], q_ps[0][:], ACT.Copy, scale=-STEP)
+        nc.scalar.activation(before[:, :, LEAD + HALF : LEAD + J - 1], q_ps[1][:, :, 0 : HALF - 1], ACT.Copy, scale=-STEP)
 
         tz_picked = sbuf("tz_picked", [P, PACK, J], F32)
         for t in range(PACK):
             window = tz_sb[t // 2][:, (t % 2) * M : (t % 2 + 1) * M]
             nc.scalar.activation(tz_picked[:, t, :], window.indirect(list_tz[:]), ACT.Copy)
 
-        stepped = [sbuf(f"stepped{h}", [P, HALF, PACK], F32) for h in range(2)]
-        hid = [sbuf(f"hid{h}", [P, HALF, PACK], BF16) for h in range(2)]
+        stepped = [sbuf(f"stepped{h}", [P, PACK, HALF], F32) for h in range(2)]
+        hid = [sbuf(f"hid{h}", [P, HALF * PACK], BF16) for h in range(2)]
         for h in range(2):
-            nc.vector.tensor_tensor(stepped[h][:], woven_view(q_ps[h]), before[:, halves[h], :], ALU.add)
+            shifted = before[:, :, LEAD - 1 + h * HALF : LEAD - 1 + (h + 1) * HALF]
+            nc.vector.tensor_tensor(stepped[h][:], q_ps[h][:], shifted, ALU.add)
         for h in range(2):
-            nc.vector.tensor_tensor(hid[h][:], woven_view(a_ps[h]), stepped[h][:], ALU.max)
+            nc.vector.tensor_tensor(
+                hid[h][:].rearrange("p (c i t) -> p c t i", i=2, t=PACK),
+                a_ps[h][:].rearrange("p t (c i) -> p c t i", i=2),
+                stepped[h][:].rearrange("p t (c i) -> p c t i", i=2),
+                ALU.max,
+            )
         p_ps = []
         for h in range(2):
             codes = sbuf(f"hid_codes{h}", [P, HALF], I32)
             scales = sbuf(f"hid_scales{h}", [P, HALF], U8)
-            nc.vector.quantize_mx(
-                out=codes[:].bitcast(E5M2), scales=scales[:], in_=hid[h][:].rearrange("p j t -> p (j t)")
-            )
+            nc.vector.quantize_mx(out=codes[:].bitcast(E5M2), scales=scales[:], in_=hid[h][:])
             p_ps.append(product(f"p_ps{h}", wb_dealt, wb_plane, E4M3, codes[:].bitcast(E5M2), scales[:]))
 
         floored = [sbuf(f"floored{h}", [P, PACK, HALF], F32) for h in range(2)]

@@ -101,28 +101,30 @@ def tile_list_two_picked_gated_stepgap_floored_pl_kernel(
         for h in range(2):
             nc.tensor.transpose(rw_ps[:, halves[h]], rw_cols[:, h : h + 1].to_broadcast([P, P]), ident[:])
 
+        def pick_planes(picked, windows, offsets, by_halves):
+            whole = PACK - by_halves
+            for t in range(whole):
+                nc.scalar.activation(picked[:, t, :], windows[t].indirect(offsets[:]), ACT.Copy)
+            for h in range(2):
+                cols = slice(h * LIST_COLS // 2, (h + 1) * LIST_COLS // 2)
+                for t in range(whole, PACK):
+                    nc.scalar.activation(picked[:, t, halves[h]], windows[t].indirect(offsets[:, cols]), ACT.Copy)
+
+        def combine_and_weave(woven, in0, in1, op):
+            nc.vector.tensor_tensor(
+                woven.rearrange("p (c i t) -> p c t i", i=2, t=PACK),
+                in0.rearrange("p t (c i) -> p c t i", i=2),
+                in1.rearrange("p t (c i) -> p c t i", i=2),
+                op,
+            )
+
         gate = sbuf("gate", [P, PACK * J], F32)
         nc.scalar.activation(gate[:], so_sb[:], ACT.Sigmoid)
-        last = PACK - 1
-        gate_last = sbuf("gate_last", [P, J], F32)
-        nc.vector.tensor_scalar(gate_last[:], gate[:, last * J :], fl_sb[:, last : last + 1], None, ALU.mult)
-        u2 = sbuf("u2", [P, 2, PACK, HALF], F32)
-        for t in range(last):
-            xo_picked = sbuf(f"xo_picked{t}", [P, J], F32)
-            nc.scalar.activation(xo_picked[:], xo_planes[t].indirect(list_xo[:]), ACT.Copy)
-            nc.vector.scalar_tensor_tensor(
-                u2[:, :, t, :],
-                xo_picked[:].rearrange("p (h j) -> p h j", h=2),
-                fl_sb[:, t : t + 1],
-                gate[:, t * J : (t + 1) * J].rearrange("p (h j) -> p h j", h=2),
-                ALU.mult,
-                ALU.mult,
-            )
-        for h in range(2):
-            cols = slice(h * LIST_COLS // 2, (h + 1) * LIST_COLS // 2)
-            nc.vector.tensor_tensor(
-                u2[:, h, last, :], xo_planes[last].indirect(list_xo[:, cols]), gate_last[:, halves[h]], ALU.mult
-            )
+        factor = sbuf("factor", [P, PACK, J], F32)
+        for t in range(PACK):
+            nc.vector.tensor_scalar(factor[:, t, :], gate[:, t * J : (t + 1) * J], fl_sb[:, t : t + 1], None, ALU.mult)
+        xo_picked = sbuf("xo_picked", [P, PACK, J], F32)
+        pick_planes(xo_picked, xo_planes, list_xo, 1)
 
         late_raw = sbuf("late_raw", [P, R + N], I32, tag="raw")
         w_raw, wb_raw = late_raw[:, 0:R], late_raw[:, R:]
@@ -144,58 +146,58 @@ def tile_list_two_picked_gated_stepgap_floored_pl_kernel(
         def round_and_weave(copy, woven, src):
             copy(woven.rearrange("p (c i t) -> p c t i", i=4, t=PACK), src.rearrange("p t (c i) -> p c t i", i=4))
 
-        def product(name, w_dealt, w_pl, w_fmt, codes, code_scales):
-            bank = ps.tile([P, PACK, HALF], F32, name=name)
-            for t in range(PACK):
+        def product(name, w_dealt, w_pl, w_fmt, codes, code_scales, slices=range(PACK)):
+            bank = ps.tile([P, len(slices), HALF], F32, name=name)
+            for i, t in enumerate(slices):
                 cols = slice(t * P, (t + 1) * P)
                 nc.tensor.matmul_mx(
-                    out=bank[:, t, :], lhsT=w_dealt[:, cols].bitcast(w_fmt), lhsT_scale=w_pl[:, cols],
+                    out=bank[:, i, :], lhsT=w_dealt[:, cols].bitcast(w_fmt), lhsT_scale=w_pl[:, cols],
                     rhs=codes, rhs_scale=code_scales, start=True, stop=True,
                 )
             return bank
 
         u2_woven = [sbuf(f"u2_woven{h}", [P, HALF * PACK], BF16) for h in range(2)]
-        for h in range(2):
-            round_and_weave(nc.scalar.copy, u2_woven[h][:], u2[:, h, :, :])
-        w2_dealt = deal_columns("w2_dealt", w2_raw[:])
+        q_banks = ([range(PACK)], [range(0, PACK // 2), range(PACK // 2, PACK)])
         q_ps = []
         for h in range(2):
+            combine_and_weave(u2_woven[h][:], xo_picked[:, :, halves[h]], factor[:, :, halves[h]], ALU.mult)
+            if h == 0:
+                w2_dealt = deal_columns("w2_dealt", w2_raw[:])
             codes = sbuf(f"u2_codes{h}", [P, HALF], I32)
             scales = sbuf(f"u2_scales{h}", [P, HALF], U8)
             nc.vector.quantize_mx(out=codes[:].bitcast(E4M3), scales=scales[:], in_=u2_woven[h][:])
-            q_ps.append(product(f"q_ps{h}", w2_dealt, w2_plane, E5M2, codes[:].bitcast(E4M3), scales[:]))
+            for slices in q_banks[h]:
+                name = f"q_ps{h}_{slices.start}"
+                bank = product(name, w2_dealt, w2_plane, E5M2, codes[:].bitcast(E4M3), scales[:], slices)
+                q_ps.append((h, slice(slices.start, slices.stop), bank))
 
         w_dealt = deal_columns("w_dealt", w_raw, tag="u2_woven1")
         a_ps = [
             product(f"a_ps{h}", w_dealt, w_plane, E5M2, xt_picked[:, halves[h]].bitcast(E2M1), xt_plane[:, halves[h]])
             for h in range(2)
         ]
-        wb_dealt = deal_columns("wb_dealt", wb_raw)
 
         before = sbuf("before", [P, PACK, LEAD + J], F32)
         nc.vector.memset(before[:, :, LEAD - 1 : LEAD], 0.0)
-        nc.scalar.activation(before[:, :, LEAD : LEAD + HALF], q_ps[0][:], ACT.Copy, scale=-STEP)
-        nc.scalar.activation(before[:, :, LEAD + HALF : LEAD + J - 1], q_ps[1][:, :, 0 : HALF - 1], ACT.Copy, scale=-STEP)
+        for h, rows, bank in q_ps:
+            first = LEAD + h * HALF
+            count = min(HALF, J - 1 - h * HALF)
+            nc.scalar.activation(before[:, rows, first : first + count], bank[:, :, 0:count], ACT.Copy, scale=-STEP)
 
         tz_picked = sbuf("tz_picked", [P, PACK, J], F32)
-        for t in range(PACK):
-            window = tz_sb[t // 2][:, (t % 2) * M : (t % 2 + 1) * M]
-            nc.scalar.activation(tz_picked[:, t, :], window.indirect(list_tz[:]), ACT.Copy)
+        tz_planes = [tz_sb[t // 2][:, (t % 2) * M : (t % 2 + 1) * M] for t in range(PACK)]
+        pick_planes(tz_picked, tz_planes, list_tz, 2)
 
         stepped = [sbuf(f"stepped{h}", [P, PACK, HALF], F32) for h in range(2)]
         hid = [sbuf(f"hid{h}", [P, HALF * PACK], BF16) for h in range(2)]
-        for h in range(2):
-            shifted = before[:, :, LEAD - 1 + h * HALF : LEAD - 1 + (h + 1) * HALF]
-            nc.vector.tensor_tensor(stepped[h][:], q_ps[h][:], shifted, ALU.add)
-        for h in range(2):
-            nc.vector.tensor_tensor(
-                hid[h][:].rearrange("p (c i t) -> p c t i", i=2, t=PACK),
-                a_ps[h][:].rearrange("p t (c i) -> p c t i", i=2),
-                stepped[h][:].rearrange("p t (c i) -> p c t i", i=2),
-                ALU.max,
-            )
+        for h, rows, bank in q_ps:
+            first = LEAD - 1 + h * HALF
+            nc.vector.tensor_tensor(stepped[h][:, rows, :], bank[:], before[:, rows, first : first + HALF], ALU.add)
         p_ps = []
         for h in range(2):
+            combine_and_weave(hid[h][:], a_ps[h][:], stepped[h][:], ALU.max)
+            if h == 0:
+                wb_dealt = deal_columns("wb_dealt", wb_raw, tag="before")
             codes = sbuf(f"hid_codes{h}", [P, HALF], I32)
             scales = sbuf(f"hid_scales{h}", [P, HALF], U8)
             nc.vector.quantize_mx(out=codes[:].bitcast(E5M2), scales=scales[:], in_=hid[h][:])
@@ -208,7 +210,6 @@ def tile_list_two_picked_gated_stepgap_floored_pl_kernel(
         y_scales = sbuf("y_scales", [P, J], U8)
         for h in range(2):
             nc.vector.tensor_tensor(floored[h][:], p_ps[h][:], tz_picked[:, :, halves[h]], ALU.max)
-        for h in range(2):
             rw_all = rw_ps[:, halves[h]].unsqueeze(1).to_broadcast([P, PACK, HALF])
             nc.vector.tensor_tensor(y[h][:], floored[h][:], rw_all, ALU.mult)
             nc.sync.dma_start(out_rows[:, :, halves[h]], y[h][:])

@@ -22,7 +22,6 @@ PACK = 4
 HALF = J // 2
 LIST_COLS = J // 16
 STEP = 0.6
-SPLIT = 48
 LEAD = 4
 
 
@@ -100,6 +99,9 @@ def tile_list_two_picked_gated_stepgap_floored_pl_kernel(
         rw_ps = ps.tile([P, J], F32, name="rw_ps")
         for h in range(2):
             nc.tensor.transpose(rw_ps[:, halves[h]], rw_cols[:, h : h + 1].to_broadcast([P, P]), ident[:])
+
+        rw_first = sbuf("rw_first", [P, HALF], F32)
+        nc.scalar.copy(rw_first[:], rw_ps[:, halves[0]])
 
         def pick_planes(picked, windows, offsets, by_halves):
             whole = PACK - by_halves
@@ -210,17 +212,20 @@ def tile_list_two_picked_gated_stepgap_floored_pl_kernel(
         y_scales = sbuf("y_scales", [P, J], U8)
         for h in range(2):
             nc.vector.tensor_tensor(floored[h][:], p_ps[h][:], tz_picked[:, :, halves[h]], ALU.max)
-            rw_all = rw_ps[:, halves[h]].unsqueeze(1).to_broadcast([P, PACK, HALF])
-            nc.vector.tensor_tensor(y[h][:], floored[h][:], rw_all, ALU.mult)
+            engine, rw_half = ((nc.gpsimd, rw_first[:]), (nc.vector, rw_ps[:, halves[1]]))[h]
+            engine.tensor_tensor(y[h][:], floored[h][:], rw_half.unsqueeze(1).to_broadcast([P, PACK, HALF]), ALU.mult)
             nc.sync.dma_start(out_rows[:, :, halves[h]], y[h][:])
         y_woven = [sbuf(f"y_woven{h}", [P, HALF * PACK], BF16) for h in range(2)]
-        round_and_weave(nc.scalar.copy, y_woven[0][:], y[0][:])
-        round_and_weave(nc.scalar.copy, y_woven[1][:, 0 : SPLIT * PACK], y[1][:, :, 0:SPLIT])
-        round_and_weave(nc.vector.tensor_copy, y_woven[1][:, SPLIT * PACK :], y[1][:, :, SPLIT:])
-        for h in range(2):
+
+        def quantize_y(h):
             nc.vector.quantize_mx(
                 out=y_codes[:, halves[h]].bitcast(E4M3), scales=y_scales[:, halves[h]], in_=y_woven[h][:]
             )
+
+        round_and_weave(nc.scalar.copy, y_woven[0][:], y[0][:])
+        round_and_weave(nc.vector.tensor_copy, y_woven[1][:], y[1][:])
+        quantize_y(0)
+        quantize_y(1)
         nc.sync.dma_start(word_rows(out_1), y_codes[:])
         for q in range(4):
             queue = nc.scalar if q % 2 == 0 else nc.sync

from contextlib import ExitStack

import concourse.mybir as mybir
from concourse.masks import make_identity

K, T, J, R, F, Z, N, M = 512, 512, 256, 512, 512, 1024, 512, 512
FLOPS = 2 * J * (K * R + F * R + R * N)

F32 = mybir.dt.float32
BF16 = mybir.dt.bfloat16
I32 = mybir.dt.int32
U16 = mybir.dt.uint16
U8 = mybir.dt.uint8
E4M3 = mybir.dt.float8_e4m3fn_x4
E5M2 = mybir.dt.float8_e5m2_x4
E2M1 = mybir.dt.float4_e2m1fn_x4
ALU = mybir.AluOpType
ACT = mybir.ActivationFunctionType

P = 128
PACK = 4
HALF = J // 2
LIST_COLS = J // 16
STEP = 0.6
LEAD = 4


def tile_list_two_picked_gated_stepgap_floored_pl_kernel(
    tc, xt_words, xt_scales, w_words, w_scales, xo, fl, so, w2_words, w2_scales,
    wb_words, wb_scales, tz, rw, offs, offs2, offs3, out_0, out_1, out_2,
):
    nc = tc.nc
    halves = [slice(h * HALF, (h + 1) * HALF) for h in range(2)]

    with ExitStack() as ctx:
        sb = ctx.enter_context(tc.tile_pool(name="sb", bufs=1))
        ps = ctx.enter_context(tc.psum_pool(name="ps", bufs=1))

        def sbuf(name, shape, dtype, tag=None):
            return sb.tile(shape, dtype, name=name, tag=tag or name, align_bytes=64)

        def word_rows(words):
            return words[0].rearrange("p c r -> p (c r)").bitcast(I32)

        list_xt = sbuf("list_xt", [P, LIST_COLS], U16)
        list_xo = sbuf("list_xo", [P, LIST_COLS], U16)
        list_tz = sbuf("list_tz", [P, LIST_COLS], U16)

        raw_scales = sbuf("raw_scales", [P, 3 * R], U8, tag="raw")
        xt_scale_rows = sbuf("xt_scale_rows", [P, T], U8)
        nc.gpsimd.memset(xt_scale_rows[:].bitcast(I32), 0)
        nc.gpsimd.memset(raw_scales[:].bitcast(I32), 0)

        so_sb = sbuf("so_sb", [P, PACK * J], F32)
        xo_rows = xo.rearrange("(p t) z -> p t z", t=PACK)
        xo_first = sbuf("xo_first", [P, 2 * Z], F32)
        xo_third = sbuf("xo_third", [P, Z], F32)
        xo_last = sbuf("xo_last", [P, Z], F32)
        xo_planes = [xo_first[:, 0:Z], xo_first[:, Z:], xo_third[:], xo_last[:]]
        xt_sb = sbuf("xt_sb", [P, T], U16)
        w2_raw = sbuf("w2_raw", [P, R], I32)
        nc.sync.dma_start(so_sb[:], so.rearrange("(p t) j -> p (t j)", t=PACK))
        nc.sync.dma_start(list_xt[:], offs)
        nc.scalar.dma_start(xt_scale_rows[0:16, :].bitcast(I32), xt_scales[0].bitcast(I32))
        for i, (src, queue) in enumerate(((w2_scales, nc.scalar), (w_scales, nc.scalar), (wb_scales, nc.sync))):
            queue.dma_start(raw_scales[0:16, i * R : (i + 1) * R].bitcast(I32), src[0].bitcast(I32))
        nc.sync.dma_start(xo_first[:], xo_rows[:, 0:2, :].rearrange("p t z -> p (t z)"))
        nc.sync.dma_start(list_xo[:], offs2)
        fl_sb = sbuf("fl_sb", [P, PACK], F32)
        nc.sync.dma_start(fl_sb[:], fl.rearrange("(p t) o -> p (t o)", t=PACK))
        nc.sync.dma_start(xt_sb[:].bitcast(I32), xt_words[0].bitcast(I32))
        nc.sync.dma_start(xo_third[:], xo_rows[:, 2, :])
        nc.sync.dma_start(xo_last[:], xo_rows[:, 3, :])
        nc.sync.dma_start(w2_raw[:], word_rows(w2_words))
        nc.sync.dma_start(list_tz[:], offs3)

        rw_cols = sbuf("rw_cols", [P, 2], F32)
        with nc.allow_non_contiguous_dma(reason="one slot weight to a partition"):
            nc.gpsimd.dma_start(rw_cols[:], rw.rearrange("o (h p) -> p (o h)", h=2))

        planes = sbuf("planes", [P, 3 * R + J], U8)
        xt_scale_picked = sbuf("xt_scale_picked", [P, J], U8)
        nc.vector.tensor_copy(xt_scale_picked[:], xt_scale_rows[:].indirect(list_xt[:]))
        nc.vector.tensor_copy(planes[:, 3 * R :].bitcast(I32), xt_scale_picked[:].bitcast(I32))
        nc.vector.tensor_copy(
            planes[:, 0 : 3 * R].rearrange("p (w t m) -> p t w m", w=3, t=PACK),
            raw_scales[:].rearrange("p (w m t) -> p t w m", w=3, t=PACK),
        )
        for q in range(1, 4):
            nc.sync.dma_start(planes[32 * q : 32 * q + 4, :].bitcast(I32), planes[4 * q : 4 * q + 4, :].bitcast(I32))
        w2_plane, w_plane, wb_plane = [planes[:, i * R : (i + 1) * R] for i in range(3)]
        xt_plane = planes[:, 3 * R :]

        xt_picked = sbuf("xt_picked", [P, J], U16)
        nc.vector.tensor_copy(xt_picked[:], xt_sb[:].indirect(list_xt[:]))

        ident = sbuf("ident", [P, P], F32)
        make_identity(nc, ident[:])
        rw_ps = ps.tile([P, J], F32, name="rw_ps")
        for h in range(2):
            nc.tensor.transpose(rw_ps[:, halves[h]], rw_cols[:, h : h + 1].to_broadcast([P, P]), ident[:])

        rw_first = sbuf("rw_first", [P, HALF], F32)
        nc.scalar.copy(rw_first[:], rw_ps[:, halves[0]])

        def pick_planes(picked, windows, offsets, by_halves):
            whole = PACK - by_halves
            for t in range(whole):
                nc.scalar.activation(picked[:, t, :], windows[t].indirect(offsets[:]), ACT.Copy)
            for h in range(2):
                cols = slice(h * LIST_COLS // 2, (h + 1) * LIST_COLS // 2)
                for t in range(whole, PACK):
                    nc.scalar.activation(picked[:, t, halves[h]], windows[t].indirect(offsets[:, cols]), ACT.Copy)

        def combine_and_weave(woven, in0, in1, op):
            nc.vector.tensor_tensor(
                woven.rearrange("p (c i t) -> p c t i", i=2, t=PACK),
                in0.rearrange("p t (c i) -> p c t i", i=2),
                in1.rearrange("p t (c i) -> p c t i", i=2),
                op,
            )

        gate = sbuf("gate", [P, PACK * J], F32)
        nc.scalar.activation(gate[:], so_sb[:], ACT.Sigmoid)
        factor = sbuf("factor", [P, PACK, J], F32)
        for t in range(PACK):
            nc.vector.tensor_scalar(factor[:, t, :], gate[:, t * J : (t + 1) * J], fl_sb[:, t : t + 1], None, ALU.mult)
        xo_picked = sbuf("xo_picked", [P, PACK, J], F32)
        pick_planes(xo_picked, xo_planes, list_xo, 1)

        late_raw = sbuf("late_raw", [P, R + N], I32, tag="raw")
        w_raw, wb_raw = late_raw[:, 0:R], late_raw[:, R:]
        tz_rows = tz.rearrange("(p u t) m -> p u (t m)", u=2, t=2)
        tz_sb = [sbuf(f"tz_sb{u}", [P, 2 * M], F32, tag=tag) for u, tag in enumerate(("xo_first", "xo_third"))]
        nc.sync.dma_start(w_raw, word_rows(w_words))
        nc.sync.dma_start(wb_raw, word_rows(wb_words))
        for u in range(2):
            nc.sync.dma_start(tz_sb[u][:], tz_rows[:, u, :])

        def deal_columns(name, raw, tag=None):
            dealt = sbuf(name, [P, R], I32, tag=tag)
            nc.vector.tensor_copy(
                dealt[:].rearrange("p (t c i) -> p c t i", t=PACK, i=4),
                raw.rearrange("p (c i t) -> p c t i", t=PACK, i=4),
            )
            return dealt

        def round_and_weave(copy, woven, src):
            copy(woven.rearrange("p (c i t) -> p c t i", i=4, t=PACK), src.rearrange("p t (c i) -> p c t i", i=4))

        def product(name, w_dealt, w_pl, w_fmt, codes, code_scales, slices=range(PACK)):
            bank = ps.tile([P, len(slices), HALF], F32, name=name)
            for i, t in enumerate(slices):
                cols = slice(t * P, (t + 1) * P)
                nc.tensor.matmul_mx(
                    out=bank[:, i, :], lhsT=w_dealt[:, cols].bitcast(w_fmt), lhsT_scale=w_pl[:, cols],
                    rhs=codes, rhs_scale=code_scales, start=True, stop=True,
                )
            return bank

        u2_woven = [sbuf(f"u2_woven{h}", [P, HALF * PACK], BF16) for h in range(2)]
        q_banks = ([range(PACK)], [range(0, PACK // 2), range(PACK // 2, PACK)])
        q_ps = []
        for h in range(2):
            combine_and_weave(u2_woven[h][:], xo_picked[:, :, halves[h]], factor[:, :, halves[h]], ALU.mult)
            if h == 0:
                w2_dealt = deal_columns("w2_dealt", w2_raw[:])
            codes = sbuf(f"u2_codes{h}", [P, HALF], I32)
            scales = sbuf(f"u2_scales{h}", [P, HALF], U8)
            nc.vector.quantize_mx(out=codes[:].bitcast(E4M3), scales=scales[:], in_=u2_woven[h][:])
            for slices in q_banks[h]:
                name = f"q_ps{h}_{slices.start}"
                bank = product(name, w2_dealt, w2_plane, E5M2, codes[:].bitcast(E4M3), scales[:], slices)
                q_ps.append((h, slice(slices.start, slices.stop), bank))

        w_dealt = deal_columns("w_dealt", w_raw, tag="u2_woven1")
        a_ps = [
            product(f"a_ps{h}", w_dealt, w_plane, E5M2, xt_picked[:, halves[h]].bitcast(E2M1), xt_plane[:, halves[h]])
            for h in range(2)
        ]

        before = sbuf("before", [P, PACK, LEAD + J], F32)
        nc.vector.memset(before[:, :, LEAD - 1 : LEAD], 0.0)
        for h, rows, bank in q_ps:
            first = LEAD + h * HALF
            count = min(HALF, J - 1 - h * HALF)
            nc.scalar.activation(before[:, rows, first : first + count], bank[:, :, 0:count], ACT.Copy, scale=-STEP)

        tz_picked = sbuf("tz_picked", [P, PACK, J], F32)
        tz_planes = [tz_sb[t // 2][:, (t % 2) * M : (t % 2 + 1) * M] for t in range(PACK)]
        pick_planes(tz_picked, tz_planes, list_tz, 2)

        stepped = [sbuf(f"stepped{h}", [P, PACK, HALF], F32) for h in range(2)]
        hid = [sbuf(f"hid{h}", [P, HALF * PACK], BF16) for h in range(2)]
        for h, rows, bank in q_ps:
            first = LEAD - 1 + h * HALF
            nc.vector.tensor_tensor(stepped[h][:, rows, :], bank[:], before[:, rows, first : first + HALF], ALU.add)
        p_ps = []
        for h in range(2):
            combine_and_weave(hid[h][:], a_ps[h][:], stepped[h][:], ALU.max)
            if h == 0:
                wb_dealt = deal_columns("wb_dealt", wb_raw, tag="before")
            codes = sbuf(f"hid_codes{h}", [P, HALF], I32)
            scales = sbuf(f"hid_scales{h}", [P, HALF], U8)
            nc.vector.quantize_mx(out=codes[:].bitcast(E5M2), scales=scales[:], in_=hid[h][:])
            p_ps.append(product(f"p_ps{h}", wb_dealt, wb_plane, E4M3, codes[:].bitcast(E5M2), scales[:]))

        floored = [sbuf(f"floored{h}", [P, PACK, HALF], F32) for h in range(2)]
        y = [sbuf(f"y{h}", [P, PACK, HALF], F32) for h in range(2)]
        out_rows = out_0.rearrange("(p t) j -> p t j", t=PACK)
        y_codes = sbuf("y_codes", [P, J], I32)
        y_scales = sbuf("y_scales", [P, J], U8)
        for h in range(2):
            nc.vector.tensor_tensor(floored[h][:], p_ps[h][:], tz_picked[:, :, halves[h]], ALU.max)
            engine, rw_half = ((nc.gpsimd, rw_first[:]), (nc.vector, rw_ps[:, halves[1]]))[h]
            engine.tensor_tensor(y[h][:], floored[h][:], rw_half.unsqueeze(1).to_broadcast([P, PACK, HALF]), ALU.mult)
            nc.sync.dma_start(out_rows[:, :, halves[h]], y[h][:])
        y_woven = [sbuf(f"y_woven{h}", [P, HALF * PACK], BF16) for h in range(2)]

        def quantize_y(h):
            nc.vector.quantize_mx(
                out=y_codes[:, halves[h]].bitcast(E4M3), scales=y_scales[:, halves[h]], in_=y_woven[h][:]
            )

        round_and_weave(nc.scalar.copy, y_woven[0][:], y[0][:])
        round_and_weave(nc.vector.tensor_copy, y_woven[1][:], y[1][:])
        quantize_y(0)
        quantize_y(1)
        nc.sync.dma_start(word_rows(out_1), y_codes[:])
        for q in range(4):
            queue = nc.scalar if q % 2 == 0 else nc.sync
            queue.dma_start(out_2[0, 4 * q : 4 * q + 4, :].bitcast(I32), y_scales[32 * q : 32 * q + 4, :].bitcast(I32))
